import numpy as np
import ml_dtypes


def mxq(x, axis, fmt="e4m3"):
    dtype, down = {"e4m3": (ml_dtypes.float8_e4m3fn, 7), "e5m2": (ml_dtypes.float8_e5m2, 14)}[fmt]
    v = np.moveaxis(np.asarray(x, np.float32).astype(ml_dtypes.bfloat16).astype(np.float64), axis, -1)
    blocks = v.reshape(v.shape[:-1] + (-1, 32))
    amax = np.abs(blocks).max(-1, keepdims=True)
    byte = np.maximum(np.where(amax > 0, np.frexp(amax)[1] - 1 + 127, 0) - down, 1)
    scale = np.exp2(byte - 127.0)
    codes = (blocks / scale).astype(np.float32).astype(dtype).astype(np.float64)
    return np.moveaxis((codes * scale).reshape(v.shape), -1, axis)


WIDE = False


def mx_kscale(k):
    if not WIDE:
        return np.ones(k)
    levels = np.array([10, -10, 5, -5, 0])
    if k % 512:
        return np.exp2(np.random.permutation(np.resize(levels, k // 32))).repeat(32)
    a = np.empty((k // 512, 16))
    for p in range(k // 512):
        a[p, :8] = np.random.permutation(np.resize(levels, 8))
        for g in range(8):
            far = levels[np.abs(levels - a[p, g]) >= 10]
            a[p, g + 8] = far[np.random.randint(len(far))]
    return np.exp2(a.ravel()).repeat(32)


def f64(x):
    return np.asarray(x).astype(np.float64)


def striped(idx):
    return np.tile(idx.reshape(-1, 16).T, (8, 1)).astype(np.uint16)


def unstriped(offs):
    return offs[:16].T.reshape(-1).astype(np.int64)


E2M1 = np.array([0.0, 0.5, 1.0, 1.5, 2.0, 3.0, 4.0, 6.0, -0.0, -0.5, -1.0, -1.5, -2.0, -3.0, -4.0, -6.0])


def pack_weight(w, fmt):
    k, n = w.shape
    w = f64(np.asarray(w, np.float32).astype(ml_dtypes.bfloat16)).reshape(k // 32, 32, n)
    amax = np.abs(w).max(1)
    if fmt == "e4m3":
        byte = np.frexp(amax)[1] - 1 + 127 - 7
    else:
        mant, ex = np.frexp(amax / 6.0)
        byte = np.where(mant > 0.5, ex, ex - 1) + 127
    byte = np.clip(np.where(amax > 0, byte, 1), 1, 254)
    scaled = (w * np.exp2(127.0 - byte)[:, None, :]).reshape(k, n).astype(np.float32)
    by_word = np.ascontiguousarray(scaled.reshape(k // 512, 128, 4, n).transpose(0, 1, 3, 2))
    if fmt == "e4m3":
        words = by_word.astype(ml_dtypes.float8_e4m3fn).view(np.uint8)
    else:
        c = by_word.astype(ml_dtypes.float4_e2m1fn).view(np.uint8) & 0xF
        words = (c[..., 0::2] | (c[..., 1::2] << 4)).reshape(k // 512, 128, 2 * n)
    return np.ascontiguousarray(words), np.ascontiguousarray(byte.astype(np.uint8).reshape(k // 512, 16, n))


def unpack_weight(words, scales, fmt):
    g, _, n = scales.shape
    words = np.ascontiguousarray(words).reshape(g, 128, n, -1)
    if fmt == "e4m3":
        vals = words.view(ml_dtypes.float8_e4m3fn).astype(np.float64)
    else:
        nib = np.empty((g, 128, n, 4), np.uint8)
        nib[..., 0::2] = words & 0xF
        nib[..., 1::2] = words >> 4
        vals = E2M1[nib]
    vals = vals * np.repeat(np.exp2(scales.astype(np.float64) - 127.0), 8, axis=1)[..., None]
    return vals.transpose(0, 1, 3, 2).reshape(g * 512, n)


def gelu(v):
    return 0.5 * v * (1.0 + np.tanh(np.sqrt(2.0 / np.pi) * (v + 0.044715 * v**3)))


def twice(P):
    return np.random.permutation(np.repeat(np.arange(P), 2))


def bf(x):
    return np.asarray(x, np.float32).astype(ml_dtypes.bfloat16)


def planes(Y):
    n, m = Y.shape
    b = f64(bf(Y)).reshape(n // 32, 32, m)
    amax = np.abs(b).max(1)
    byte = np.clip(np.where(amax > 0, np.frexp(amax)[1] - 1 + 127 - 7, 1), 1, 254)
    codes = (b * np.exp2(127.0 - byte)[:, None, :]).reshape(n, m).astype(np.float32).astype(ml_dtypes.float8_e4m3fn).view(np.uint8)
    words = codes.reshape(n // 512, 128, 4, m).transpose(0, 1, 3, 2)
    return np.ascontiguousarray(words), np.ascontiguousarray(byte.astype(np.uint8).reshape(n // 512, 16, m))


K, H, T, S, P = 1024, 1024, 4096, 1024, 512

def setup_inputs():
    n = np.random.standard_normal
    s = mx_kscale(K)[:, None]
    u = mx_kscale(H)[:, None]
    ro = np.exp(0.8 * n(H))
    d = {}
    d["tab_words"], d["tab_scales"] = pack_weight(n((K, T)) * s, "e4m3")
    d["offs"] = striped(np.random.permutation(T)[:S])
    d["w1"] = (n((K, H)) / K**0.5 / s * u.T).astype(np.float32)
    d["pos1"] = striped(np.random.permutation(S)[:P])
    d["pos2"] = striped(np.random.permutation(S)[:P])
    d["w2_words"], d["w2_scales"] = pack_weight(n((H, H)) / H**0.5 / u, "e2m1")
    d["gain"] = (np.exp(0.3 * n(H)) * u[:, 0]).astype(np.float32)
    d["w3"] = (1.3 * n((H, H)) / H**0.5 / u * ro[None, :]).astype(np.float32)
    d["pos3"] = striped(twice(P))
    d["lim"] = (ro * (0.3 + 0.4 * n(H))).astype(np.float32)
    d["wh"] = (0.7 * ro / u[:, 0]).astype(np.float32)
    return d

def reference(tab_words, tab_scales, offs, w1, pos1, pos2, w2_words, w2_scales, gain, w3, pos3, lim, wh):
    v = unpack_weight(tab_words, tab_scales, "e4m3")[:, unstriped(offs)]
    h = mxq(f64(w1), 0, "e4m3").T @ v
    x = mxq(h[:, unstriped(pos1)] + h[:, unstriped(pos2)], 0, "e4m3")
    w2 = unpack_weight(w2_words, w2_scales, "e2m1")
    th = np.tanh(w2.T @ x)
    tq = mxq(f64(gain)[:, None] * th, 0, "e4m3")
    box = (mxq(f64(w3), 0, "e4m3").T @ tq) - th
    up = box[:, unstriped(pos3)]
    y = np.minimum(up, f64(lim)[:, None]) + f64(wh)[:, None] * h
    words, scales = planes(y)
    return y, words, scales

@@ -1,0 +1,322 @@
+from contextlib import ExitStack
+
+import concourse.mybir as mybir
+
+F32 = mybir.dt.float32
+BF16 = mybir.dt.bfloat16
+I32 = mybir.dt.int32
+U32 = mybir.dt.uint32
+U16 = mybir.dt.uint16
+U8 = mybir.dt.uint8
+FP8X4 = mybir.dt.float8_e4m3fn_x4
+FP4X4 = mybir.dt.float4_e2m1fn_x4
+ALU = mybir.AluOpType
+ACT = mybir.ActivationFunctionType
+
+FLOPS = 4294967296
+
+P = 128
+T = 4096
+S = 1024
+B = 512
+PAD = 32
+
+
+def tile_list_vanilla_pod_features_kernel(
+    tc, tab_words, tab_scales, offs, w1, pos1, pos2, w2_words, w2_scales, gain, w3, pos3, lim, wh, out_0, out_1, out_2
+):
+    nc = tc.nc
+    with ExitStack() as ctx:
+        keep = ctx.enter_context(tc.tile_pool(name="keep", bufs=1))
+        ring = ctx.enter_context(tc.tile_pool(name="ring", bufs=1))
+        psum = ctx.enter_context(tc.psum_pool(name="psum", bufs=8))
+
+        offs_sb = keep.tile([P, S // 16], U16, name="offs_sb")
+        pos1_sb = keep.tile([P, B // 16], U16, name="pos1_sb")
+        pos2_sb = keep.tile([P, B // 16], U16, name="pos2_sb")
+        pos3_sb = keep.tile([P, S // 16], U16, name="pos3_sb")
+
+        def big(shape, dtype, name):
+            return ring.tile(shape, dtype, name=name, tag="big", bufs=2, align_bytes=64)
+
+        def raw_tile(name):
+            return ring.tile([P, 4, 512], F32, name=name, tag="raw", bufs=4, align_bytes=64)
+
+        def slot_tile(slot, name, shape=(P, 2048), dtype=BF16):
+            return ring.tile(list(shape), dtype, name=name, tag="slot" + slot, bufs=1, align_bytes=64)
+
+        def quad_tile(name):
+            return ring.tile([P, 4, 512], F32, name=name, tag="quad", bufs=2, align_bytes=64)
+
+        def tmp_tile(name):
+            return ring.tile([P, 512], F32, name=name, tag="tmp", bufs=3, align_bytes=64)
+
+        def mx_tiles(name, width):
+            codes = keep.tile([P, width], U32, name=name + "_c", align_bytes=64)
+            scales = keep.tile([P, width], U8, name=name + "_s", align_bytes=64)
+            return codes, scales
+
+        def load_w(w, a, b, name, parts=1):
+            raw = raw_tile(name)
+            width = 512 // parts
+            src = w[512 * a : 512 * a + 512, :].rearrange("(p j) c -> p j c", j=4)
+            for i in range(parts):
+                nc.sync.dma_start(
+                    out=raw[:, :, i * width : (i + 1) * width],
+                    in_=src[:, :, 512 * b + i * width : 512 * b + (i + 1) * width],
+                )
+            return raw
+
+        def deal_w(copy, dst, raw, q0, q1):
+            copy(
+                out=dst[:].rearrange("p (t q j) -> p q j t", t=4, j=4)[:, q0:q1],
+                in_=raw[:].rearrange("p j (q t) -> p q j t", t=4)[:, q0:q1],
+            )
+
+        def weave(copy, dst, src, c0, c1):
+            copy(
+                out=dst.rearrange("p (c i t) -> p c t i", i=4, t=4)[:, c0:c1],
+                in_=src.rearrange("p t (c i) -> p c t i", i=4)[:, c0:c1],
+            )
+
+        def quant(codes, scales, src):
+            nc.vector.quantize_mx(out=codes.bitcast(FP8X4), scales=scales, in_=src)
+
+        tsc = keep.tile([P, T], U8, name="tsc", align_bytes=64)
+        w2s_raw = keep.tile([P, 2, 1024], U8, name="w2s_raw", align_bytes=64)
+        nc.vector.memset(tsc[:].bitcast(I32), 0)
+        nc.vector.memset(w2s_raw[:].bitcast(I32), 0)
+        vecs = []
+        for name, v in (("gain_sb", gain), ("lim_sb", lim), ("wh_sb", wh)):
+            v_sb = keep.tile([P, 2, 4], F32, name=name)
+            nc.gpsimd.dma_start(out=v_sb[:], in_=v.rearrange("(b p t) -> p b t", b=2, t=4))
+            vecs.append(v_sb)
+        gain_sb, lim_sb, wh_sb = vecs
+        box = [keep.tile([P, B + PAD], F32, name=f"box{s}", align_bytes=64) for s in range(8)]
+        for s in range(8):
+            nc.vector.memset(box[s][:, B:], 0.0)
+
+        nc.sync.dma_start(offs_sb[:], offs)
+        w2w_raw = keep.tile([P, 2, 2048], U8, name="w2w_raw", align_bytes=64)
+        tab = [big([P, T], I32, f"tab{a}") for a in range(2)]
+        w1_raw = {}
+        nc.sync.dma_start(out=tab[0][:], in_=tab_words[0].rearrange("p n t -> p (n t)").bitcast(I32))
+        for q in range(4):
+            nc.sync.dma_start(
+                out=tsc[32 * q : 32 * q + 8, :].bitcast(I32), in_=tab_scales[:, 4 * q : 4 * q + 4, :].bitcast(I32)
+            )
+        nc.sync.dma_start(out=w2w_raw[:].bitcast(I32), in_=w2_words.rearrange("a p n -> p a n").bitcast(I32))
+        w1_raw[0, 0] = load_w(w1, 0, 0, "w1r00")
+        for q in range(4):
+            nc.sync.dma_start(
+                out=w2s_raw[32 * q : 32 * q + 4, :, :].bitcast(I32),
+                in_=w2_scales[:, 4 * q : 4 * q + 4, :].rearrange("a r n -> r a n").bitcast(I32),
+            )
+        nc.sync.dma_start(out=tab[1][:], in_=tab_words[1].rearrange("p n t -> p (n t)").bitcast(I32))
+        w1_raw[1, 0] = load_w(w1, 1, 0, "w1r10", parts=2)
+        nc.sync.dma_start(pos1_sb[:], pos1)
+        nc.sync.dma_start(pos2_sb[:], pos2)
+        w1_raw[0, 1] = load_w(w1, 0, 1, "w1r01")
+        w1_raw[1, 1] = load_w(w1, 1, 1, "w1r11")
+        nc.sync.dma_start(pos3_sb[:], pos3)
+
+        w2w = keep.tile([P, 2, 2048], U8, name="w2w", align_bytes=64)
+        w2s = keep.tile([P, 2, 1024], U8, name="w2s", align_bytes=64)
+        nc.vector.tensor_copy(
+            out=w2w[:].bitcast(U16).rearrange("p a (b t q) -> p (a b) q t", b=2, t=4),
+            in_=w2w_raw[:].bitcast(U16).rearrange("p a (b q t) -> p (a b) q t", b=2, t=4),
+        )
+
+        gs = keep.tile([P, S], U8, name="gs", align_bytes=64)
+        gw = [keep.tile([P, S], U32, name=f"gw{a}", align_bytes=64) for a in range(2)]
+        nc.vector.tensor_copy(gw[0][:], tab[0][:].bitcast(U32).indirect(offs_sb[:]))
+        nc.vector.tensor_copy(gs[:], tsc[:].indirect(offs_sb[:]))
+        nc.vector.tensor_copy(
+            out=w2s[:].rearrange("p a (b t q) -> p (a b) q t", b=2, t=4),
+            in_=w2s_raw[:].rearrange("p a (b q t) -> p (a b) q t", b=2, t=4),
+        )
+        w1q = {(a, b): mx_tiles(f"w1q{a}{b}", 512) for a in range(2) for b in range(2)}
+
+        wb = slot_tile("A", "wb00")
+        deal_w(nc.scalar.copy, wb, w1_raw[0, 0], 0, 128)
+        quant(w1q[0, 0][0][:], w1q[0, 0][1][:], wb[:])
+        nc.vector.tensor_copy(gw[1][:], tab[1][:].bitcast(U32).indirect(offs_sb[:]))
+        wb = slot_tile("B", "wb10")
+        deal_w(nc.scalar.copy, wb, w1_raw[1, 0], 0, 64)
+        deal_w(nc.vector.tensor_copy, wb, w1_raw[1, 0], 64, 128)
+        for t in range(4):
+            quant(w1q[1, 0][0][:, 128 * t : 128 * t + 128], w1q[1, 0][1][:, 128 * t : 128 * t + 128], wb[:, 512 * t : 512 * t + 512])
+
+        def mm(acc, wq, t, rhs, rhs_scale, a):
+            cols = slice(128 * t, 128 * t + 128)
+            nc.tensor.matmul_mx(
+                out=acc[:], lhsT=wq[0][:, cols].bitcast(FP8X4), lhsT_scale=wq[1][:, cols],
+                rhs=rhs.bitcast(FP8X4), rhs_scale=rhs_scale, start=(a == 0), stop=(a == 1),
+            )
+
+        h = [keep.tile([P, S], F32, name=f"h{s}", align_bytes=64) for s in range(8)]
+
+        def stage1_pass(accs, b, t, a):
+            for u in range(2):
+                cols = slice(512 * u, 512 * u + 512)
+                mm(accs[t, u], w1q[a, b], t, gw[a][:, cols], gs[4 * a : P, cols], a)
+
+        xq = [mx_tiles(f"xq{b}", 512) for b in range(2)]
+        xf = [quad_tile(f"x{b}") for b in range(2)]
+        w3_raw = {}
+
+        def pair_sum(b, t, first):
+            nc.vector.tensor_copy(first[:], h[4 * b + t][:].indirect(pos1_sb[:]))
+            nc.vector.tensor_tensor(xf[b][:, t, :], h[4 * b + t][:].indirect(pos2_sb[:]), first[:], ALU.add)
+
+        def finish_h(accs, b, t):
+            stage1_pass(accs, b, t, 1)
+            for u in range(2):
+                copy = nc.vector.tensor_copy if (b, t, u) == (0, 0, 1) else nc.scalar.copy
+                copy(out=h[4 * b + t][:, 512 * u : 512 * u + 512], in_=accs[t, u][:])
+
+        def open_h(b):
+            accs = {(t, u): psum.tile([P, 512], F32, name=f"acc1_{b}{t}{u}", tag="acc") for t in range(4) for u in range(2)}
+            for t in range(4):
+                stage1_pass(accs, b, t, 0)
+            return accs
+
+        accs = open_h(0)
+        finish_h(accs, 0, 0)
+        pair_sum(0, 0, tmp_tile("first0"))
+        finish_h(accs, 0, 1)
+        pair_sum(0, 1, tmp_tile("first1"))
+        wb01 = slot_tile("A", "wb01")
+        deal_w(nc.scalar.copy, wb01, w1_raw[0, 1], 0, 64)
+        finish_h(accs, 0, 2)
+        pair_sum(0, 2, tmp_tile("first2"))
+        deal_w(nc.scalar.copy, wb01, w1_raw[0, 1], 64, 128)
+        quant(w1q[0, 1][0][:], w1q[0, 1][1][:], wb01[:])
+        wb11 = slot_tile("B", "wb11")
+        deal_w(nc.scalar.copy, wb11, w1_raw[1, 1], 0, 64)
+        finish_h(accs, 0, 3)
+        deal_w(nc.scalar.copy, wb11, w1_raw[1, 1], 64, 128)
+        quant(w1q[1, 1][0][:], w1q[1, 1][1][:], wb11[:])
+        pair_sum(0, 3, slot_tile("B", "first3", (P, 512), F32))
+        for bb in range(2):
+            for a in range(2):
+                w3_raw[a, bb] = load_w(w3, a, bb, f"w3r{a}{bb}")
+        accs = open_h(1)
+        for t in range(4):
+            finish_h(accs, 1, t)
+            if t == 0:
+                first = slot_tile("A", "first4", (P, 512), F32)
+            elif t == 3:
+                first = slot_tile("E", "first7", (P, 512), F32)
+            else:
+                first = tmp_tile(f"first{4 + t}")
+            pair_sum(1, t, first)
+
+        xb = slot_tile("A", "xb0")
+        weave(nc.scalar.copy, xb[:], xf[0][:], 0, 128)
+        quant(xq[0][0][:], xq[0][1][:], xb[:])
+        w3b = {}
+        for key, slot in (((0, 0), "C"), ((1, 0), "D")):
+            w3b[key] = slot_tile(slot, f"w3b{key[0]}{key[1]}")
+            deal_w(nc.scalar.copy, w3b[key], w3_raw[key], 0, 128)
+        xb = slot_tile("B", "xb1")
+        weave(nc.vector.tensor_copy, xb[:], xf[1][:], 0, 84)
+        weave(nc.scalar.copy, xb[:], xf[1][:], 84, 128)
+        quant(xq[1][0][:], xq[1][1][:], xb[:])
+        w3c0 = slot_tile("E", "w3c0", (P, 1024), U32)
+        w3q = {}
+        for a in range(2):
+            w3q[a, 0] = (w3c0[:, 512 * a : 512 * a + 512], keep.tile([P, 512], U8, name=f"w3s{a}0", align_bytes=64))
+            w3q[a, 1] = mx_tiles(f"w3q{a}1", 512)
+
+        accs = [psum.tile([P, 512], F32, name=f"acc2_{s}", tag="acc") for s in range(8)]
+
+        def mm2(s, a):
+            nc.tensor.matmul_mx(
+                out=accs[s][:], lhsT=w2w[:, a, 256 * s : 256 * s + 256].bitcast(FP4X4),
+                lhsT_scale=w2s[:, a, 128 * s : 128 * s + 128],
+                rhs=xq[a][0][:].bitcast(FP8X4), rhs_scale=xq[a][1][:], start=(a == 0), stop=(a == 1),
+            )
+
+        for s in range(8):
+            mm2(s, 0)
+        th = [quad_tile(f"th{b}") for b in range(2)]
+        for s in range(8):
+            mm2(s, 1)
+            nc.scalar.activation(out=th[s // 4][:, s % 4, :], in_=accs[s][:], func=ACT.Tanh)
+        for key in ((0, 0), (1, 0)):
+            quant(w3q[key][0][:], w3q[key][1][:], w3b[key][:])
+        w3b[0, 1] = slot_tile("B", "w3b01")
+        deal_w(nc.vector.tensor_copy, w3b[0, 1], w3_raw[0, 1], 0, 128)
+        tq = [mx_tiles(f"tq{b}", 512) for b in range(2)]
+        for b in range(2):
+            tb = slot_tile("AC"[b], f"tb{b}")
+            nc.vector.tensor_tensor(
+                tb[:].rearrange("p (c i t) -> p c t i", i=4, t=4),
+                th[b][:].rearrange("p t (c i) -> p c t i", i=4),
+                gain_sb[:, b, :].unsqueeze(1).unsqueeze(3).to_broadcast([P, 128, 4, 4]),
+                ALU.mult,
+            )
+            quant(tq[b][0][:], tq[b][1][:], tb[:])
+        quant(w3q[0, 1][0][:], w3q[0, 1][1][:], w3b[0, 1][:])
+        w3b[1, 1] = slot_tile("D", "w3b11")
+        deal_w(nc.scalar.copy, w3b[1, 1], w3_raw[1, 1], 0, 128)
+
+        yq = [keep.tile([P, S], U32, name=f"yq{b}", align_bytes=64) for b in range(2)]
+        ys = keep.tile([P, 2, S], U8, name="ys", align_bytes=64)
+        y = [big([P, 4, S], F32, f"y{b}") for b in range(2)]
+
+        def stage3(b):
+            accs3 = [psum.tile([P, 512], F32, name=f"acc3_{b}{t}", tag="acc") for t in range(4)]
+            for t in range(4):
+                mm(accs3[t], w3q[0, b], t, tq[0][0][:], tq[0][1][:], 0)
+            for t in range(4):
+                mm(accs3[t], w3q[1, b], t, tq[1][0][:], tq[1][1][:], 1)
+                diff = tmp_tile(f"diff{b}{t}")
+                nc.vector.tensor_tensor(diff[:], accs3[t][:], th[b][:, t, :], ALU.subtract)
+                nc.vector.tensor_scalar(box[4 * b + t][:, 0:B], diff[:], lim_sb[:, b, t : t + 1], None, ALU.min)
+
+        def join(b, u):
+            cols = slice(512 * u, 512 * u + 512)
+            y_out = out_0[512 * b : 512 * b + 512, :].rearrange("(p t) j -> p t j", t=4)
+            for t in range(4):
+                own = ring.tile([P, 512], F32, name=f"own{b}{u}{t}", tag="own", bufs=4, align_bytes=64)
+                nc.scalar.activation(out=own[:], in_=h[4 * b + t][:, cols], func=ACT.Copy, scale=wh_sb[:, b, t : t + 1])
+                nc.vector.tensor_tensor(
+                    y[b][:, t, cols], box[4 * b + t][:].indirect(pos3_sb[:, 32 * u : 32 * u + 32]), own[:], ALU.add
+                )
+                if (b, u) == (1, 1):
+                    nc.sync.dma_start(out=y_out[:, t, cols], in_=y[b][:, t, cols])
+            if (b, u) != (1, 1):
+                nc.sync.dma_start(out=y_out[:, :, cols], in_=y[b][:, :, cols])
+
+        def planes(b, u):
+            cols = slice(512 * u, 512 * u + 512)
+            yb = slot_tile("AB"[u], f"yb{b}{u}")
+            if (b, u) == (1, 1):
+                weave(nc.vector.tensor_copy, yb[:], y[b][:, :, cols], 0, 84)
+                weave(nc.scalar.copy, yb[:], y[b][:, :, cols], 84, 128)
+            else:
+                weave(nc.scalar.copy, yb[:], y[b][:, :, cols], 0, 128)
+            quant(yq[b][:, cols], ys[:, b, cols], yb[:])
+            nc.sync.dma_start(
+                out=out_1[b].rearrange("p m t -> p (m t)").bitcast(I32)[:, cols], in_=yq[b][:, cols].bitcast(I32)
+            )
+
+        stage3(0)
+        join(0, 0)
+        quant(w3q[1, 1][0][:], w3q[1, 1][1][:], w3b[1, 1][:])
+        stage3(1)
+        join(0, 1)
+        planes(0, 0)
+        join(1, 0)
+        planes(0, 1)
+        join(1, 1)
+        planes(1, 0)
+        planes(1, 1)
+        for q in range(4):
+            queue = nc.sync if q % 2 == 0 else nc.scalar
+            queue.dma_start(
+                out=out_2[:, 4 * q : 4 * q + 4, :].rearrange("g r m -> r g m").bitcast(I32),
+                in_=ys[32 * q : 32 * q + 4, :, :].bitcast(I32),
+            )

@@ -16,10 +16,14 @@ ACT = mybir.ActivationFunctionType
 FLOPS = 4294967296
 
 P = 128
-T = 4096
-S = 1024
-B = 512
-PAD = 32
+GROUP = 512
+CHANNELS = 1024
+TABLE = 4096
+BUNDLES = 1024
+BOXES = 512
+BANK = 512
+BOX_SPARE = 32
+VECTOR_SHARE = 42 / 64
 
 
 def tile_list_vanilla_pod_features_kernel(
@@ -28,295 +32,323 @@ def tile_list_vanilla_pod_features_kernel(
     nc = tc.nc
     with ExitStack() as ctx:
         keep = ctx.enter_context(tc.tile_pool(name="keep", bufs=1))
-        ring = ctx.enter_context(tc.tile_pool(name="ring", bufs=1))
+        shared = ctx.enter_context(tc.tile_pool(name="shared", bufs=1))
         psum = ctx.enter_context(tc.psum_pool(name="psum", bufs=8))
 
-        offs_sb = keep.tile([P, S // 16], U16, name="offs_sb")
-        pos1_sb = keep.tile([P, B // 16], U16, name="pos1_sb")
-        pos2_sb = keep.tile([P, B // 16], U16, name="pos2_sb")
-        pos3_sb = keep.tile([P, S // 16], U16, name="pos3_sb")
+        offs_sb = keep.tile([P, BUNDLES // 16], U16, name="offs_sb")
+        pos1_sb = keep.tile([P, BOXES // 16], U16, name="pos1_sb")
+        pos2_sb = keep.tile([P, BOXES // 16], U16, name="pos2_sb")
+        pos3_sb = keep.tile([P, BUNDLES // 16], U16, name="pos3_sb")
 
-        def big(shape, dtype, name):
-            return ring.tile(shape, dtype, name=name, tag="big", bufs=2, align_bytes=64)
+        def wide_tile(shape, dtype, name):
+            return shared.tile(shape, dtype, name=name, tag="wide", bufs=2, align_bytes=64)
 
-        def raw_tile(name):
-            return ring.tile([P, 4, 512], F32, name=name, tag="raw", bufs=4, align_bytes=64)
+        def load_tile(a, b, name, dtype=F32):
+            return shared.tile([P, 4, GROUP], dtype, name=name, tag=f"load{a}{b}", bufs=1, align_bytes=64)
 
-        def slot_tile(slot, name, shape=(P, 2048), dtype=BF16):
-            return ring.tile(list(shape), dtype, name=name, tag="slot" + slot, bufs=1, align_bytes=64)
+        def stage_tile(place, name, shape=(P, 4 * GROUP), dtype=BF16):
+            return shared.tile(list(shape), dtype, name=name, tag="stage" + place, bufs=1, align_bytes=64)
 
-        def quad_tile(name):
-            return ring.tile([P, 4, 512], F32, name=name, tag="quad", bufs=2, align_bytes=64)
+        def planes_tile(name):
+            return shared.tile([P, 4, BOXES], F32, name=name, tag="planes", bufs=2, align_bytes=64)
 
-        def tmp_tile(name):
-            return ring.tile([P, 512], F32, name=name, tag="tmp", bufs=3, align_bytes=64)
+        def plane_tile(name):
+            return shared.tile([P, BOXES], F32, name=name, tag="plane", bufs=3, align_bytes=64)
 
-        def mx_tiles(name, width):
-            codes = keep.tile([P, width], U32, name=name + "_c", align_bytes=64)
-            scales = keep.tile([P, width], U8, name=name + "_s", align_bytes=64)
+        def bank_tile(name):
+            return psum.tile([P, BANK], F32, name=name, tag="bank")
+
+        def mx_tiles(name):
+            codes = keep.tile([P, GROUP], U32, name=name + "_codes", align_bytes=64)
+            scales = keep.tile([P, GROUP], U8, name=name + "_scales", align_bytes=64)
             return codes, scales
 
-        def load_w(w, a, b, name, parts=1):
-            raw = raw_tile(name)
-            width = 512 // parts
-            src = w[512 * a : 512 * a + 512, :].rearrange("(p j) c -> p j c", j=4)
+        def load_weight(w, a, b, name, parts=1):
+            block = load_tile(a, b, name)
+            width = GROUP // parts
+            rows = w[GROUP * a : GROUP * (a + 1), :].rearrange("(p j) c -> p j c", j=4)
             for i in range(parts):
                 nc.sync.dma_start(
-                    out=raw[:, :, i * width : (i + 1) * width],
-                    in_=src[:, :, 512 * b + i * width : 512 * b + (i + 1) * width],
+                    out=block[:, :, i * width : (i + 1) * width],
+                    in_=rows[:, :, GROUP * b + i * width : GROUP * b + (i + 1) * width],
                 )
-            return raw
+            return block
 
-        def deal_w(copy, dst, raw, q0, q1):
+        def load_scale_rows(tile, scales):
+            for quad in range(4):
+                nc.sync.dma_start(
+                    out=tile[32 * quad : 32 * quad + 4, :, :].bitcast(I32),
+                    in_=scales[:, 4 * quad : 4 * quad + 4, :].rearrange("a r n -> r a n").bitcast(I32),
+                )
+
+        def deal_weight(copy, dst, block, q0=0, q1=P):
             copy(
                 out=dst[:].rearrange("p (t q j) -> p q j t", t=4, j=4)[:, q0:q1],
-                in_=raw[:].rearrange("p j (q t) -> p q j t", t=4)[:, q0:q1],
+                in_=block[:].rearrange("p j (q t) -> p q j t", t=4)[:, q0:q1],
             )
 
-        def weave(copy, dst, src, c0, c1):
+        def interleave(copy, dst, src, c0, c1):
             copy(
                 out=dst.rearrange("p (c i t) -> p c t i", i=4, t=4)[:, c0:c1],
                 in_=src.rearrange("p t (c i) -> p c t i", i=4)[:, c0:c1],
             )
 
-        def quant(codes, scales, src):
+        def interleave_on_both(dst, src, columns):
+            split = round(VECTOR_SHARE * columns / 4)
+            interleave(nc.vector.tensor_copy, dst, src, 0, split)
+            interleave(nc.scalar.copy, dst, src, split, columns // 4)
+
+        def quantize(codes, scales, src):
             nc.vector.quantize_mx(out=codes.bitcast(FP8X4), scales=scales, in_=src)
 
-        tsc = keep.tile([P, T], U8, name="tsc", align_bytes=64)
-        w2s_raw = keep.tile([P, 2, 1024], U8, name="w2s_raw", align_bytes=64)
-        nc.vector.memset(tsc[:].bitcast(I32), 0)
-        nc.vector.memset(w2s_raw[:].bitcast(I32), 0)
-        vecs = []
-        for name, v in (("gain_sb", gain), ("lim_sb", lim), ("wh_sb", wh)):
-            v_sb = keep.tile([P, 2, 4], F32, name=name)
-            nc.gpsimd.dma_start(out=v_sb[:], in_=v.rearrange("(b p t) -> p b t", b=2, t=4))
-            vecs.append(v_sb)
-        gain_sb, lim_sb, wh_sb = vecs
-        box = [keep.tile([P, B + PAD], F32, name=f"box{s}", align_bytes=64) for s in range(8)]
-        for s in range(8):
-            nc.vector.memset(box[s][:, B:], 0.0)
+        def fp8_pass(bank, weight, t, codes, scales, a):
+            cols = slice(P * t, P * (t + 1))
+            nc.tensor.matmul_mx(
+                out=bank[:],
+                lhsT=weight[0][:, cols].bitcast(FP8X4),
+                lhsT_scale=weight[1][:, cols],
+                rhs=codes.bitcast(FP8X4),
+                rhs_scale=scales,
+                start=(a == 0),
+                stop=(a == 1),
+            )
 
+        tab_scales_sb = keep.tile([P, 2, TABLE], U8, name="tab_scales_sb", align_bytes=64)
+        w2_scales_sb = keep.tile([P, 2, CHANNELS], U8, name="w2_scales_sb", align_bytes=64)
+        nc.gpsimd.memset(tab_scales_sb[:, 1, :].bitcast(I32), 0)
+        nc.vector.memset(tab_scales_sb[:, 0, :].bitcast(I32), 0)
+        nc.vector.memset(w2_scales_sb[:].bitcast(I32), 0)
+        box = [keep.tile([P, BOXES + BOX_SPARE], F32, name=f"box{s}", align_bytes=64) for s in range(8)]
+        for plane in box:
+            nc.vector.memset(plane[:, BOXES:], 0.0)
+
+        w2_words_sb = keep.tile([P, 2, 2 * CHANNELS], U8, name="w2_words_sb", align_bytes=64)
+        tab_sb = [wide_tile([P, TABLE], I32, f"tab_sb{a}") for a in range(2)]
+        w1_sb = {}
         nc.sync.dma_start(offs_sb[:], offs)
-        w2w_raw = keep.tile([P, 2, 2048], U8, name="w2w_raw", align_bytes=64)
-        tab = [big([P, T], I32, f"tab{a}") for a in range(2)]
-        w1_raw = {}
-        nc.sync.dma_start(out=tab[0][:], in_=tab_words[0].rearrange("p n t -> p (n t)").bitcast(I32))
-        for q in range(4):
-            nc.sync.dma_start(
-                out=tsc[32 * q : 32 * q + 8, :].bitcast(I32), in_=tab_scales[:, 4 * q : 4 * q + 4, :].bitcast(I32)
-            )
-        nc.sync.dma_start(out=w2w_raw[:].bitcast(I32), in_=w2_words.rearrange("a p n -> p a n").bitcast(I32))
-        w1_raw[0, 0] = load_w(w1, 0, 0, "w1r00")
-        for q in range(4):
-            nc.sync.dma_start(
-                out=w2s_raw[32 * q : 32 * q + 4, :, :].bitcast(I32),
-                in_=w2_scales[:, 4 * q : 4 * q + 4, :].rearrange("a r n -> r a n").bitcast(I32),
-            )
-        nc.sync.dma_start(out=tab[1][:], in_=tab_words[1].rearrange("p n t -> p (n t)").bitcast(I32))
-        w1_raw[1, 0] = load_w(w1, 1, 0, "w1r10", parts=2)
+        nc.sync.dma_start(out=w2_words_sb[:].bitcast(I32), in_=w2_words.rearrange("a p n -> p a n").bitcast(I32))
         nc.sync.dma_start(pos1_sb[:], pos1)
         nc.sync.dma_start(pos2_sb[:], pos2)
-        w1_raw[0, 1] = load_w(w1, 0, 1, "w1r01")
-        w1_raw[1, 1] = load_w(w1, 1, 1, "w1r11")
+        load_scale_rows(tab_scales_sb, tab_scales)
+        nc.sync.dma_start(out=tab_sb[0][:], in_=tab_words[0].rearrange("p n t -> p (n t)").bitcast(I32))
+        load_scale_rows(w2_scales_sb, w2_scales)
+        w1_sb[0, 0] = load_weight(w1, 0, 0, "w1_sb00")
+        nc.sync.dma_start(out=tab_sb[1][:], in_=tab_words[1].rearrange("p n t -> p (n t)").bitcast(I32))
+        w1_sb[1, 0] = load_weight(w1, 1, 0, "w1_sb10", parts=2)
+        w1_sb[0, 1] = load_weight(w1, 0, 1, "w1_sb01")
+        w1_sb[1, 1] = load_weight(w1, 1, 1, "w1_sb11")
         nc.sync.dma_start(pos3_sb[:], pos3)
 
-        w2w = keep.tile([P, 2, 2048], U8, name="w2w", align_bytes=64)
-        w2s = keep.tile([P, 2, 1024], U8, name="w2s", align_bytes=64)
+        w2_codes = keep.tile([P, 2, 2 * CHANNELS], U8, name="w2_codes", align_bytes=64)
+        w2_bytes = keep.tile([P, 2, CHANNELS], U8, name="w2_bytes", align_bytes=64)
+        v_scales = [keep.tile([P, BUNDLES], U8, name=f"v_scales{a}", align_bytes=64) for a in range(2)]
+        v_codes = [keep.tile([P, BUNDLES], U32, name=f"v_codes{a}", align_bytes=64) for a in range(2)]
         nc.vector.tensor_copy(
-            out=w2w[:].bitcast(U16).rearrange("p a (b t q) -> p (a b) q t", b=2, t=4),
-            in_=w2w_raw[:].bitcast(U16).rearrange("p a (b q t) -> p (a b) q t", b=2, t=4),
+            out=w2_codes[:].bitcast(U16).rearrange("p a (b t q) -> p (a b) t q", b=2, t=4),
+            in_=w2_words_sb[:].bitcast(U16).rearrange("p a (b q t) -> p (a b) t q", b=2, t=4),
         )
-
-        gs = keep.tile([P, S], U8, name="gs", align_bytes=64)
-        gw = [keep.tile([P, S], U32, name=f"gw{a}", align_bytes=64) for a in range(2)]
-        nc.vector.tensor_copy(gw[0][:], tab[0][:].bitcast(U32).indirect(offs_sb[:]))
-        nc.vector.tensor_copy(gs[:], tsc[:].indirect(offs_sb[:]))
-        nc.vector.tensor_copy(
-            out=w2s[:].rearrange("p a (b t q) -> p (a b) q t", b=2, t=4),
-            in_=w2s_raw[:].rearrange("p a (b q t) -> p (a b) q t", b=2, t=4),
-        )
-        w1q = {(a, b): mx_tiles(f"w1q{a}{b}", 512) for a in range(2) for b in range(2)}
-
-        wb = slot_tile("A", "wb00")
-        deal_w(nc.scalar.copy, wb, w1_raw[0, 0], 0, 128)
-        quant(w1q[0, 0][0][:], w1q[0, 0][1][:], wb[:])
-        nc.vector.tensor_copy(gw[1][:], tab[1][:].bitcast(U32).indirect(offs_sb[:]))
-        wb = slot_tile("B", "wb10")
-        deal_w(nc.scalar.copy, wb, w1_raw[1, 0], 0, 64)
-        deal_w(nc.vector.tensor_copy, wb, w1_raw[1, 0], 64, 128)
-        for t in range(4):
-            quant(w1q[1, 0][0][:, 128 * t : 128 * t + 128], w1q[1, 0][1][:, 128 * t : 128 * t + 128], wb[:, 512 * t : 512 * t + 512])
-
-        def mm(acc, wq, t, rhs, rhs_scale, a):
-            cols = slice(128 * t, 128 * t + 128)
-            nc.tensor.matmul_mx(
-                out=acc[:], lhsT=wq[0][:, cols].bitcast(FP8X4), lhsT_scale=wq[1][:, cols],
-                rhs=rhs.bitcast(FP8X4), rhs_scale=rhs_scale, start=(a == 0), stop=(a == 1),
-            )
-
-        h = [keep.tile([P, S], F32, name=f"h{s}", align_bytes=64) for s in range(8)]
-
-        def stage1_pass(accs, b, t, a):
-            for u in range(2):
-                cols = slice(512 * u, 512 * u + 512)
-                mm(accs[t, u], w1q[a, b], t, gw[a][:, cols], gs[4 * a : P, cols], a)
-
-        xq = [mx_tiles(f"xq{b}", 512) for b in range(2)]
-        xf = [quad_tile(f"x{b}") for b in range(2)]
-        w3_raw = {}
-
-        def pair_sum(b, t, first):
-            nc.vector.tensor_copy(first[:], h[4 * b + t][:].indirect(pos1_sb[:]))
-            nc.vector.tensor_tensor(xf[b][:, t, :], h[4 * b + t][:].indirect(pos2_sb[:]), first[:], ALU.add)
-
-        def finish_h(accs, b, t):
-            stage1_pass(accs, b, t, 1)
-            for u in range(2):
-                copy = nc.vector.tensor_copy if (b, t, u) == (0, 0, 1) else nc.scalar.copy
-                copy(out=h[4 * b + t][:, 512 * u : 512 * u + 512], in_=accs[t, u][:])
-
-        def open_h(b):
-            accs = {(t, u): psum.tile([P, 512], F32, name=f"acc1_{b}{t}{u}", tag="acc") for t in range(4) for u in range(2)}
-            for t in range(4):
-                stage1_pass(accs, b, t, 0)
-            return accs
-
-        accs = open_h(0)
-        finish_h(accs, 0, 0)
-        pair_sum(0, 0, tmp_tile("first0"))
-        finish_h(accs, 0, 1)
-        pair_sum(0, 1, tmp_tile("first1"))
-        wb01 = slot_tile("A", "wb01")
-        deal_w(nc.scalar.copy, wb01, w1_raw[0, 1], 0, 64)
-        finish_h(accs, 0, 2)
-        pair_sum(0, 2, tmp_tile("first2"))
-        deal_w(nc.scalar.copy, wb01, w1_raw[0, 1], 64, 128)
-        quant(w1q[0, 1][0][:], w1q[0, 1][1][:], wb01[:])
-        wb11 = slot_tile("B", "wb11")
-        deal_w(nc.scalar.copy, wb11, w1_raw[1, 1], 0, 64)
-        finish_h(accs, 0, 3)
-        deal_w(nc.scalar.copy, wb11, w1_raw[1, 1], 64, 128)
-        quant(w1q[1, 1][0][:], w1q[1, 1][1][:], wb11[:])
-        pair_sum(0, 3, slot_tile("B", "first3", (P, 512), F32))
-        for bb in range(2):
-            for a in range(2):
-                w3_raw[a, bb] = load_w(w3, a, bb, f"w3r{a}{bb}")
-        accs = open_h(1)
-        for t in range(4):
-            finish_h(accs, 1, t)
-            if t == 0:
-                first = slot_tile("A", "first4", (P, 512), F32)
-            elif t == 3:
-                first = slot_tile("E", "first7", (P, 512), F32)
-            else:
-                first = tmp_tile(f"first{4 + t}")
-            pair_sum(1, t, first)
-
-        xb = slot_tile("A", "xb0")
-        weave(nc.scalar.copy, xb[:], xf[0][:], 0, 128)
-        quant(xq[0][0][:], xq[0][1][:], xb[:])
-        w3b = {}
-        for key, slot in (((0, 0), "C"), ((1, 0), "D")):
-            w3b[key] = slot_tile(slot, f"w3b{key[0]}{key[1]}")
-            deal_w(nc.scalar.copy, w3b[key], w3_raw[key], 0, 128)
-        xb = slot_tile("B", "xb1")
-        weave(nc.vector.tensor_copy, xb[:], xf[1][:], 0, 84)
-        weave(nc.scalar.copy, xb[:], xf[1][:], 84, 128)
-        quant(xq[1][0][:], xq[1][1][:], xb[:])
-        w3c0 = slot_tile("E", "w3c0", (P, 1024), U32)
-        w3q = {}
         for a in range(2):
-            w3q[a, 0] = (w3c0[:, 512 * a : 512 * a + 512], keep.tile([P, 512], U8, name=f"w3s{a}0", align_bytes=64))
-            w3q[a, 1] = mx_tiles(f"w3q{a}1", 512)
+            nc.vector.tensor_copy(v_scales[a][:], tab_scales_sb[:, a, :].indirect(offs_sb[:]))
+        nc.vector.tensor_copy(v_codes[0][:], tab_sb[0][:].bitcast(U32).indirect(offs_sb[:]))
+        nc.vector.tensor_copy(
+            out=w2_bytes[:].rearrange("p a (b t q) -> p (a b) t q", b=2, t=4),
+            in_=w2_scales_sb[:].rearrange("p a (b q t) -> p (a b) t q", b=2, t=4),
+        )
 
-        accs = [psum.tile([P, 512], F32, name=f"acc2_{s}", tag="acc") for s in range(8)]
+        w1_mx = {(a, b): mx_tiles(f"w1_mx{a}{b}") for a in range(2) for b in range(2)}
+        w1_bf00 = stage_tile("A", "w1_bf00")
+        deal_weight(nc.scalar.copy, w1_bf00, w1_sb[0, 0])
+        quantize(w1_mx[0, 0][0][:], w1_mx[0, 0][1][:], w1_bf00[:])
+        nc.vector.tensor_copy(v_codes[1][:], tab_sb[1][:].bitcast(U32).indirect(offs_sb[:]))
+        w1_bf10 = stage_tile("B", "w1_bf10")
+        deal_weight(nc.scalar.copy, w1_bf10, w1_sb[1, 0], 0, P // 2)
+        deal_weight(nc.vector.tensor_copy, w1_bf10, w1_sb[1, 0], P // 2, P)
+        for t in range(4):
+            cols = slice(P * t, P * (t + 1))
+            quantize(w1_mx[1, 0][0][:, cols], w1_mx[1, 0][1][:, cols], w1_bf10[:, GROUP * t : GROUP * (t + 1)])
 
-        def mm2(s, a):
+        h = [keep.tile([P, BUNDLES], F32, name=f"h{s}", align_bytes=64) for s in range(8)]
+        x_mx = [mx_tiles(f"x_mx{g}") for g in range(2)]
+        x = [planes_tile(f"x{g}") for g in range(2)]
+
+        def make_h(g, t):
+            banks = [bank_tile(f"h_bank{g}{t}{u}") for u in range(2)]
+            for a in range(2):
+                for u in range(2):
+                    cols = slice(BANK * u, BANK * (u + 1))
+                    fp8_pass(banks[u], w1_mx[a, g], t, v_codes[a][:, cols], v_scales[a][:, cols], a)
+            for u in range(2):
+                copy = nc.vector.tensor_copy if (g, t, u) == (0, 0, 1) else nc.scalar.copy
+                copy(out=h[4 * g + t][:, BANK * u : BANK * (u + 1)], in_=banks[u][:])
+
+        def make_x(g, t, first):
+            window = h[4 * g + t]
+            half = BOXES // 2
+            for u in range(2):
+                entries = pos1_sb[:, half // 16 * u : half // 16 * (u + 1)]
+                nc.vector.tensor_copy(first[:, half * u : half * (u + 1)], window[:].indirect(entries))
+            for u in range(2):
+                cols = slice(half * u, half * (u + 1))
+                entries = pos2_sb[:, half // 16 * u : half // 16 * (u + 1)]
+                nc.vector.tensor_tensor(x[g][:, t, cols], window[:].indirect(entries), first[:, cols], ALU.add)
+
+        make_h(0, 0)
+        make_x(0, 0, plane_tile("first0"))
+        make_h(0, 1)
+        make_x(0, 1, plane_tile("first1"))
+        w1_bf01 = stage_tile("A", "w1_bf01")
+        deal_weight(nc.scalar.copy, w1_bf01, w1_sb[0, 1], 0, P // 2)
+        make_h(0, 2)
+        make_x(0, 2, plane_tile("first2"))
+        deal_weight(nc.scalar.copy, w1_bf01, w1_sb[0, 1], P // 2, P)
+        quantize(w1_mx[0, 1][0][:], w1_mx[0, 1][1][:], w1_bf01[:])
+        w1_bf11 = stage_tile("B", "w1_bf11")
+        deal_weight(nc.scalar.copy, w1_bf11, w1_sb[1, 1], 0, P // 2)
+        make_h(0, 3)
+        deal_weight(nc.vector.tensor_copy, w1_bf11, w1_sb[1, 1], P // 2, P)
+        quantize(w1_mx[1, 1][0][:], w1_mx[1, 1][1][:], w1_bf11[:])
+        make_x(0, 3, stage_tile("B", "first3", (P, BOXES), F32))
+        w3_sb = {(a, b): load_weight(w3, a, b, f"w3_sb{a}{b}") for b in range(2) for a in range(2)}
+        gain_sb = keep.tile([P, 2, 4], F32, name="gain_sb")
+        lim_sb = keep.tile([P, 2, 4], F32, name="lim_sb")
+        wh_sb = keep.tile([P, 2, 4], F32, name="wh_sb")
+        for tile, vector in ((gain_sb, gain), (lim_sb, lim), (wh_sb, wh)):
+            nc.sync.dma_start(out=tile[:], in_=vector.rearrange("(g p t) -> p g t", g=2, t=4))
+
+        make_h(1, 0)
+        make_x(1, 0, stage_tile("A", "first4", (P, BOXES), F32))
+        make_h(1, 1)
+        make_x(1, 1, stage_tile("E", "first5", (P, BOXES), F32))
+        make_h(1, 2)
+        make_x(1, 2, plane_tile("first6"))
+        make_h(1, 3)
+        x_bf0 = stage_tile("A", "x_bf0")
+        interleave(nc.scalar.copy, x_bf0[:], x[0][:], 0, BOXES // 4)
+        quantize(x_mx[0][0][:], x_mx[0][1][:], x_bf0[:])
+        make_x(1, 3, stage_tile("A", "first7", (P, BOXES), F32))
+
+        w3_bf = {}
+        for a, place in ((0, "C"), (1, "E")):
+            w3_bf[a, 0] = stage_tile(place, f"w3_bf{a}0")
+            deal_weight(nc.scalar.copy, w3_bf[a, 0], w3_sb[a, 0])
+        x_bf1 = stage_tile("B", "x_bf1")
+        interleave_on_both(x_bf1[:], x[1][:], BOXES)
+        quantize(x_mx[1][0][:], x_mx[1][1][:], x_bf1[:])
+        w3_codes0 = stage_tile("A", "w3_codes0", (P, 2 * GROUP), U32)
+        w3_mx = {}
+        for a in range(2):
+            scales = keep.tile([P, GROUP], U8, name=f"w3_scales{a}0", align_bytes=64)
+            w3_mx[a, 0] = (w3_codes0[:, GROUP * a : GROUP * (a + 1)], scales)
+            w3_mx[a, 1] = mx_tiles(f"w3_mx{a}1")
+
+        th_banks = [bank_tile(f"th_bank{s}") for s in range(8)]
+
+        def fp4_pass(s, a):
             nc.tensor.matmul_mx(
-                out=accs[s][:], lhsT=w2w[:, a, 256 * s : 256 * s + 256].bitcast(FP4X4),
-                lhsT_scale=w2s[:, a, 128 * s : 128 * s + 128],
-                rhs=xq[a][0][:].bitcast(FP8X4), rhs_scale=xq[a][1][:], start=(a == 0), stop=(a == 1),
+                out=th_banks[s][:],
+                lhsT=w2_codes[:, a, 2 * P * s : 2 * P * (s + 1)].bitcast(FP4X4),
+                lhsT_scale=w2_bytes[:, a, P * s : P * (s + 1)],
+                rhs=x_mx[a][0][:].bitcast(FP8X4),
+                rhs_scale=x_mx[a][1][:],
+                start=(a == 0),
+                stop=(a == 1),
             )
 
         for s in range(8):
-            mm2(s, 0)
-        th = [quad_tile(f"th{b}") for b in range(2)]
+            fp4_pass(s, 0)
+        th = [planes_tile(f"th{g}") for g in range(2)]
+        gained = [load_tile(1 - g, 0, f"gained{g}", BF16) for g in range(2)]
         for s in range(8):
-            mm2(s, 1)
-            nc.scalar.activation(out=th[s // 4][:, s % 4, :], in_=accs[s][:], func=ACT.Tanh)
-        for key in ((0, 0), (1, 0)):
-            quant(w3q[key][0][:], w3q[key][1][:], w3b[key][:])
-        w3b[0, 1] = slot_tile("B", "w3b01")
-        deal_w(nc.vector.tensor_copy, w3b[0, 1], w3_raw[0, 1], 0, 128)
-        tq = [mx_tiles(f"tq{b}", 512) for b in range(2)]
-        for b in range(2):
-            tb = slot_tile("AC"[b], f"tb{b}")
-            nc.vector.tensor_tensor(
-                tb[:].rearrange("p (c i t) -> p c t i", i=4, t=4),
-                th[b][:].rearrange("p t (c i) -> p c t i", i=4),
-                gain_sb[:, b, :].unsqueeze(1).unsqueeze(3).to_broadcast([P, 128, 4, 4]),
-                ALU.mult,
-            )
-            quant(tq[b][0][:], tq[b][1][:], tb[:])
-        quant(w3q[0, 1][0][:], w3q[0, 1][1][:], w3b[0, 1][:])
-        w3b[1, 1] = slot_tile("D", "w3b11")
-        deal_w(nc.scalar.copy, w3b[1, 1], w3_raw[1, 1], 0, 128)
+            g, t = divmod(s, 4)
+            fp4_pass(s, 1)
+            nc.scalar.activation(out=th[g][:, t, :], in_=th_banks[s][:], func=ACT.Tanh)
+            nc.vector.tensor_scalar(gained[g][:, t, :], th[g][:, t, :], gain_sb[:, g, t : t + 1], None, ALU.mult)
+        for a in range(2):
+            quantize(w3_mx[a, 0][0][:], w3_mx[a, 0][1][:], w3_bf[a, 0][:])
+        gained_mx = [mx_tiles(f"gained_mx{g}") for g in range(2)]
+        for g, place in ((0, "D"), (1, "C")):
+            gained_bf = stage_tile(place, f"gained_bf{g}")
+            half = BOXES // 2
+            for u in range(2):
+                interleave(nc.vector.tensor_copy, gained_bf[:], gained[g][:], half // 4 * u, half // 4 * (u + 1))
+            for u in range(2):
+                cols = slice(half * u, half * (u + 1))
+                quantize(gained_mx[g][0][:, cols], gained_mx[g][1][:, cols], gained_bf[:, 4 * half * u : 4 * half * (u + 1)])
 
-        yq = [keep.tile([P, S], U32, name=f"yq{b}", align_bytes=64) for b in range(2)]
-        ys = keep.tile([P, 2, S], U8, name="ys", align_bytes=64)
-        y = [big([P, 4, S], F32, f"y{b}") for b in range(2)]
+        y_codes = [keep.tile([P, BUNDLES], U32, name=f"y_codes{g}", align_bytes=64) for g in range(2)]
+        y_scales = keep.tile([P, 2, BUNDLES], U8, name="y_scales", align_bytes=64)
+        y = [wide_tile([P, 4, BUNDLES], F32, f"y{g}") for g in range(2)]
 
-        def stage3(b):
-            accs3 = [psum.tile([P, 512], F32, name=f"acc3_{b}{t}", tag="acc") for t in range(4)]
+        def make_box(g):
+            banks = [bank_tile(f"box_bank{g}{t}") for t in range(4)]
             for t in range(4):
-                mm(accs3[t], w3q[0, b], t, tq[0][0][:], tq[0][1][:], 0)
-            for t in range(4):
-                mm(accs3[t], w3q[1, b], t, tq[1][0][:], tq[1][1][:], 1)
-                diff = tmp_tile(f"diff{b}{t}")
-                nc.vector.tensor_tensor(diff[:], accs3[t][:], th[b][:, t, :], ALU.subtract)
-                nc.vector.tensor_scalar(box[4 * b + t][:, 0:B], diff[:], lim_sb[:, b, t : t + 1], None, ALU.min)
+                fp8_pass(banks[t], w3_mx[0, g], t, gained_mx[0][0][:], gained_mx[0][1][:], 0)
+            diffs = []
 
-        def join(b, u):
-            cols = slice(512 * u, 512 * u + 512)
-            y_out = out_0[512 * b : 512 * b + 512, :].rearrange("(p t) j -> p t j", t=4)
+            def cap(t):
+                nc.vector.tensor_scalar(box[4 * g + t][:, 0:BOXES], diffs[t][:], lim_sb[:, g, t : t + 1], None, ALU.min)
+
             for t in range(4):
-                own = ring.tile([P, 512], F32, name=f"own{b}{u}{t}", tag="own", bufs=4, align_bytes=64)
-                nc.scalar.activation(out=own[:], in_=h[4 * b + t][:, cols], func=ACT.Copy, scale=wh_sb[:, b, t : t + 1])
-                nc.vector.tensor_tensor(
-                    y[b][:, t, cols], box[4 * b + t][:].indirect(pos3_sb[:, 32 * u : 32 * u + 32]), own[:], ALU.add
+                fp8_pass(banks[t], w3_mx[1, g], t, gained_mx[1][0][:], gained_mx[1][1][:], 1)
+                diffs.append(plane_tile(f"diff{g}{t}"))
+                nc.vector.tensor_tensor(diffs[t][:], banks[t][:], th[g][:, t, :], ALU.subtract)
+                if t > 0:
+                    cap(t - 1)
+            cap(3)
+
+        def scale_h(g, u):
+            own = load_tile(1, u, f"own{g}{u}")
+            for t in range(4):
+                nc.scalar.activation(
+                    out=own[:, t, :],
+                    in_=h[4 * g + t][:, GROUP * u : GROUP * (u + 1)],
+                    func=ACT.Copy,
+                    scale=wh_sb[:, g, t : t + 1],
                 )
-                if (b, u) == (1, 1):
-                    nc.sync.dma_start(out=y_out[:, t, cols], in_=y[b][:, t, cols])
-            if (b, u) != (1, 1):
-                nc.sync.dma_start(out=y_out[:, :, cols], in_=y[b][:, :, cols])
+            return own
 
-        def planes(b, u):
-            cols = slice(512 * u, 512 * u + 512)
-            yb = slot_tile("AB"[u], f"yb{b}{u}")
-            if (b, u) == (1, 1):
-                weave(nc.vector.tensor_copy, yb[:], y[b][:, :, cols], 0, 84)
-                weave(nc.scalar.copy, yb[:], y[b][:, :, cols], 84, 128)
+        def make_y(g, own, c0, c1):
+            for t in range(4):
+                nc.vector.tensor_tensor(
+                    y[g][:, t, c0:c1],
+                    box[4 * g + t][:].indirect(pos3_sb[:, c0 // 16 : c1 // 16]),
+                    own[:, t, c0 % GROUP : c0 % GROUP + c1 - c0],
+                    ALU.add,
+                )
+            rows = out_0[GROUP * g : GROUP * (g + 1), :].rearrange("(p t) j -> p t j", t=4)
+            nc.sync.dma_start(out=rows[:, :, c0:c1], in_=y[g][:, :, c0:c1])
+
+        def quantize_y(g, place, c0, c1, on_both=False):
+            y_bf = stage_tile(place, f"y_bf{g}_{c0}", (P, 4 * (c1 - c0)))
+            if on_both:
+                interleave_on_both(y_bf[:], y[g][:, :, c0:c1], c1 - c0)
             else:
-                weave(nc.scalar.copy, yb[:], y[b][:, :, cols], 0, 128)
-            quant(yq[b][:, cols], ys[:, b, cols], yb[:])
-            nc.sync.dma_start(
-                out=out_1[b].rearrange("p m t -> p (m t)").bitcast(I32)[:, cols], in_=yq[b][:, cols].bitcast(I32)
-            )
+                interleave(nc.scalar.copy, y_bf[:], y[g][:, :, c0:c1], 0, (c1 - c0) // 4)
+            quantize(y_codes[g][:, c0:c1], y_scales[:, g, c0:c1], y_bf[:])
+            words = out_1[g].rearrange("p m t -> p (m t)").bitcast(I32)
+            nc.sync.dma_start(out=words[:, c0:c1], in_=y_codes[g][:, c0:c1].bitcast(I32))
 
-        stage3(0)
-        join(0, 0)
-        quant(w3q[1, 1][0][:], w3q[1, 1][1][:], w3b[1, 1][:])
-        stage3(1)
-        join(0, 1)
-        planes(0, 0)
-        join(1, 0)
-        planes(0, 1)
-        join(1, 1)
-        planes(1, 0)
-        planes(1, 1)
-        for q in range(4):
-            queue = nc.sync if q % 2 == 0 else nc.scalar
+        half, three_quarters = BUNDLES // 2, 3 * BUNDLES // 4
+        make_box(0)
+        make_y(0, scale_h(0, 0), 0, half)
+        for a, place in ((0, "D"), (1, "C")):
+            w3_bf[a, 1] = stage_tile(place, f"w3_bf{a}1")
+            deal_weight(nc.scalar.copy, w3_bf[a, 1], w3_sb[a, 1])
+            quantize(w3_mx[a, 1][0][:], w3_mx[a, 1][1][:], w3_bf[a, 1][:])
+        make_y(0, scale_h(0, 1), half, BUNDLES)
+        make_box(1)
+        quantize_y(0, "A", 0, half)
+        make_y(1, scale_h(1, 0), 0, half)
+        quantize_y(0, "B", half, BUNDLES)
+        own_last = scale_h(1, 1)
+        make_y(1, own_last, half, three_quarters)
+        quantize_y(1, "A", 0, half)
+        make_y(1, own_last, three_quarters, BUNDLES)
+        quantize_y(1, "B", half, three_quarters)
+        quantize_y(1, "D", three_quarters, BUNDLES, on_both=True)
+        for quad in range(4):
+            queue = nc.sync if quad % 2 == 0 else nc.scalar
             queue.dma_start(
-                out=out_2[:, 4 * q : 4 * q + 4, :].rearrange("g r m -> r g m").bitcast(I32),
-                in_=ys[32 * q : 32 * q + 4, :, :].bitcast(I32),
+                out=out_2[:, 4 * quad : 4 * quad + 4, :].rearrange("g r m -> r g m").bitcast(I32),
+                in_=y_scales[32 * quad : 32 * quad + 4, :, :].bitcast(I32),
             )

from contextlib import ExitStack

import concourse.mybir as mybir

F32 = mybir.dt.float32
BF16 = mybir.dt.bfloat16
I32 = mybir.dt.int32
U32 = mybir.dt.uint32
U16 = mybir.dt.uint16
U8 = mybir.dt.uint8
FP8X4 = mybir.dt.float8_e4m3fn_x4
FP4X4 = mybir.dt.float4_e2m1fn_x4
ALU = mybir.AluOpType
ACT = mybir.ActivationFunctionType

FLOPS = 4294967296

P = 128
GROUP = 512
CHANNELS = 1024
TABLE = 4096
BUNDLES = 1024
BOXES = 512
BANK = 512
BOX_SPARE = 32
VECTOR_SHARE = 42 / 64


def tile_list_vanilla_pod_features_kernel(
    tc, tab_words, tab_scales, offs, w1, pos1, pos2, w2_words, w2_scales, gain, w3, pos3, lim, wh, out_0, out_1, out_2
):
    nc = tc.nc
    with ExitStack() as ctx:
        keep = ctx.enter_context(tc.tile_pool(name="keep", bufs=1))
        shared = ctx.enter_context(tc.tile_pool(name="shared", bufs=1))
        psum = ctx.enter_context(tc.psum_pool(name="psum", bufs=8))

        offs_sb = keep.tile([P, BUNDLES // 16], U16, name="offs_sb")
        pos1_sb = keep.tile([P, BOXES // 16], U16, name="pos1_sb")
        pos2_sb = keep.tile([P, BOXES // 16], U16, name="pos2_sb")
        pos3_sb = keep.tile([P, BUNDLES // 16], U16, name="pos3_sb")

        def wide_tile(shape, dtype, name):
            return shared.tile(shape, dtype, name=name, tag="wide", bufs=2, align_bytes=64)

        def load_tile(a, b, name, dtype=F32):
            return shared.tile([P, 4, GROUP], dtype, name=name, tag=f"load{a}{b}", bufs=1, align_bytes=64)

        def stage_tile(place, name, shape=(P, 4 * GROUP), dtype=BF16):
            return shared.tile(list(shape), dtype, name=name, tag="stage" + place, bufs=1, align_bytes=64)

        def planes_tile(name):
            return shared.tile([P, 4, BOXES], F32, name=name, tag="planes", bufs=2, align_bytes=64)

        def plane_tile(name):
            return shared.tile([P, BOXES], F32, name=name, tag="plane", bufs=3, align_bytes=64)

        def bank_tile(name):
            return psum.tile([P, BANK], F32, name=name, tag="bank")

        def mx_tiles(name):
            codes = keep.tile([P, GROUP], U32, name=name + "_codes", align_bytes=64)
            scales = keep.tile([P, GROUP], U8, name=name + "_scales", align_bytes=64)
            return codes, scales

        def load_weight(w, a, b, name, parts=1):
            block = load_tile(a, b, name)
            width = GROUP // parts
            rows = w[GROUP * a : GROUP * (a + 1), :].rearrange("(p j) c -> p j c", j=4)
            for i in range(parts):
                nc.sync.dma_start(
                    out=block[:, :, i * width : (i + 1) * width],
                    in_=rows[:, :, GROUP * b + i * width : GROUP * b + (i + 1) * width],
                )
            return block

        def load_scale_rows(tile, scales):
            for quad in range(4):
                nc.sync.dma_start(
                    out=tile[32 * quad : 32 * quad + 4, :, :].bitcast(I32),
                    in_=scales[:, 4 * quad : 4 * quad + 4, :].rearrange("a r n -> r a n").bitcast(I32),
                )

        def deal_weight(copy, dst, block, q0=0, q1=P):
            copy(
                out=dst[:].rearrange("p (t q j) -> p q j t", t=4, j=4)[:, q0:q1],
                in_=block[:].rearrange("p j (q t) -> p q j t", t=4)[:, q0:q1],
            )

        def interleave(copy, dst, src, c0, c1):
            copy(
                out=dst.rearrange("p (c i t) -> p c t i", i=4, t=4)[:, c0:c1],
                in_=src.rearrange("p t (c i) -> p c t i", i=4)[:, c0:c1],
            )

        def interleave_on_both(dst, src, columns):
            split = round(VECTOR_SHARE * columns / 4)
            interleave(nc.vector.tensor_copy, dst, src, 0, split)
            interleave(nc.scalar.copy, dst, src, split, columns // 4)

        def quantize(codes, scales, src):
            nc.vector.quantize_mx(out=codes.bitcast(FP8X4), scales=scales, in_=src)

        def fp8_pass(bank, weight, t, codes, scales, a):
            cols = slice(P * t, P * (t + 1))
            nc.tensor.matmul_mx(
                out=bank[:],
                lhsT=weight[0][:, cols].bitcast(FP8X4),
                lhsT_scale=weight[1][:, cols],
                rhs=codes.bitcast(FP8X4),
                rhs_scale=scales,
                start=(a == 0),
                stop=(a == 1),
            )

        tab_scales_sb = keep.tile([P, 2, TABLE], U8, name="tab_scales_sb", align_bytes=64)
        w2_scales_sb = keep.tile([P, 2, CHANNELS], U8, name="w2_scales_sb", align_bytes=64)
        nc.gpsimd.memset(tab_scales_sb[:, 1, :].bitcast(I32), 0)
        nc.vector.memset(tab_scales_sb[:, 0, :].bitcast(I32), 0)
        nc.vector.memset(w2_scales_sb[:].bitcast(I32), 0)
        box = [keep.tile([P, BOXES + BOX_SPARE], F32, name=f"box{s}", align_bytes=64) for s in range(8)]
        for plane in box:
            nc.vector.memset(plane[:, BOXES:], 0.0)

        w2_words_sb = keep.tile([P, 2, 2 * CHANNELS], U8, name="w2_words_sb", align_bytes=64)
        tab_sb = [wide_tile([P, TABLE], I32, f"tab_sb{a}") for a in range(2)]
        w1_sb = {}
        nc.sync.dma_start(offs_sb[:], offs)
        nc.sync.dma_start(out=w2_words_sb[:].bitcast(I32), in_=w2_words.rearrange("a p n -> p a n").bitcast(I32))
        nc.sync.dma_start(pos1_sb[:], pos1)
        nc.sync.dma_start(pos2_sb[:], pos2)
        load_scale_rows(tab_scales_sb, tab_scales)
        nc.sync.dma_start(out=tab_sb[0][:], in_=tab_words[0].rearrange("p n t -> p (n t)").bitcast(I32))
        load_scale_rows(w2_scales_sb, w2_scales)
        w1_sb[0, 0] = load_weight(w1, 0, 0, "w1_sb00")
        nc.sync.dma_start(out=tab_sb[1][:], in_=tab_words[1].rearrange("p n t -> p (n t)").bitcast(I32))
        w1_sb[1, 0] = load_weight(w1, 1, 0, "w1_sb10", parts=2)
        w1_sb[0, 1] = load_weight(w1, 0, 1, "w1_sb01")
        w1_sb[1, 1] = load_weight(w1, 1, 1, "w1_sb11")
        nc.sync.dma_start(pos3_sb[:], pos3)

        w2_codes = keep.tile([P, 2, 2 * CHANNELS], U8, name="w2_codes", align_bytes=64)
        w2_bytes = keep.tile([P, 2, CHANNELS], U8, name="w2_bytes", align_bytes=64)
        v_scales = [keep.tile([P, BUNDLES], U8, name=f"v_scales{a}", align_bytes=64) for a in range(2)]
        v_codes = [keep.tile([P, BUNDLES], U32, name=f"v_codes{a}", align_bytes=64) for a in range(2)]
        nc.vector.tensor_copy(
            out=w2_codes[:].bitcast(U16).rearrange("p a (b t q) -> p (a b) t q", b=2, t=4),
            in_=w2_words_sb[:].bitcast(U16).rearrange("p a (b q t) -> p (a b) t q", b=2, t=4),
        )
        for a in range(2):
            nc.vector.tensor_copy(v_scales[a][:], tab_scales_sb[:, a, :].indirect(offs_sb[:]))
        nc.vector.tensor_copy(v_codes[0][:], tab_sb[0][:].bitcast(U32).indirect(offs_sb[:]))
        nc.vector.tensor_copy(
            out=w2_bytes[:].rearrange("p a (b t q) -> p (a b) t q", b=2, t=4),
            in_=w2_scales_sb[:].rearrange("p a (b q t) -> p (a b) t q", b=2, t=4),
        )

        w1_mx = {(a, b): mx_tiles(f"w1_mx{a}{b}") for a in range(2) for b in range(2)}
        w1_bf00 = stage_tile("A", "w1_bf00")
        deal_weight(nc.scalar.copy, w1_bf00, w1_sb[0, 0])
        quantize(w1_mx[0, 0][0][:], w1_mx[0, 0][1][:], w1_bf00[:])
        nc.vector.tensor_copy(v_codes[1][:], tab_sb[1][:].bitcast(U32).indirect(offs_sb[:]))
        w1_bf10 = stage_tile("B", "w1_bf10")
        deal_weight(nc.scalar.copy, w1_bf10, w1_sb[1, 0], 0, P // 2)
        deal_weight(nc.vector.tensor_copy, w1_bf10, w1_sb[1, 0], P // 2, P)
        for t in range(4):
            cols = slice(P * t, P * (t + 1))
            quantize(w1_mx[1, 0][0][:, cols], w1_mx[1, 0][1][:, cols], w1_bf10[:, GROUP * t : GROUP * (t + 1)])

        h = [keep.tile([P, BUNDLES], F32, name=f"h{s}", align_bytes=64) for s in range(8)]
        x_mx = [mx_tiles(f"x_mx{g}") for g in range(2)]
        x = [planes_tile(f"x{g}") for g in range(2)]

        def make_h(g, t):
            banks = [bank_tile(f"h_bank{g}{t}{u}") for u in range(2)]
            for a in range(2):
                for u in range(2):
                    cols = slice(BANK * u, BANK * (u + 1))
                    fp8_pass(banks[u], w1_mx[a, g], t, v_codes[a][:, cols], v_scales[a][:, cols], a)
            for u in range(2):
                copy = nc.vector.tensor_copy if (g, t, u) == (0, 0, 1) else nc.scalar.copy
                copy(out=h[4 * g + t][:, BANK * u : BANK * (u + 1)], in_=banks[u][:])

        def make_x(g, t, first):
            window = h[4 * g + t]
            half = BOXES // 2
            for u in range(2):
                entries = pos1_sb[:, half // 16 * u : half // 16 * (u + 1)]
                nc.vector.tensor_copy(first[:, half * u : half * (u + 1)], window[:].indirect(entries))
            for u in range(2):
                cols = slice(half * u, half * (u + 1))
                entries = pos2_sb[:, half // 16 * u : half // 16 * (u + 1)]
                nc.vector.tensor_tensor(x[g][:, t, cols], window[:].indirect(entries), first[:, cols], ALU.add)

        make_h(0, 0)
        make_x(0, 0, plane_tile("first0"))
        make_h(0, 1)
        make_x(0, 1, plane_tile("first1"))
        w1_bf01 = stage_tile("A", "w1_bf01")
        deal_weight(nc.scalar.copy, w1_bf01, w1_sb[0, 1], 0, P // 2)
        make_h(0, 2)
        make_x(0, 2, plane_tile("first2"))
        deal_weight(nc.scalar.copy, w1_bf01, w1_sb[0, 1], P // 2, P)
        quantize(w1_mx[0, 1][0][:], w1_mx[0, 1][1][:], w1_bf01[:])
        w1_bf11 = stage_tile("B", "w1_bf11")
        deal_weight(nc.scalar.copy, w1_bf11, w1_sb[1, 1], 0, P // 2)
        make_h(0, 3)
        deal_weight(nc.vector.tensor_copy, w1_bf11, w1_sb[1, 1], P // 2, P)
        quantize(w1_mx[1, 1][0][:], w1_mx[1, 1][1][:], w1_bf11[:])
        make_x(0, 3, stage_tile("B", "first3", (P, BOXES), F32))
        w3_sb = {(a, b): load_weight(w3, a, b, f"w3_sb{a}{b}") for b in range(2) for a in range(2)}
        gain_sb = keep.tile([P, 2, 4], F32, name="gain_sb")
        lim_sb = keep.tile([P, 2, 4], F32, name="lim_sb")
        wh_sb = keep.tile([P, 2, 4], F32, name="wh_sb")
        for tile, vector in ((gain_sb, gain), (lim_sb, lim), (wh_sb, wh)):
            nc.sync.dma_start(out=tile[:], in_=vector.rearrange("(g p t) -> p g t", g=2, t=4))

        make_h(1, 0)
        make_x(1, 0, stage_tile("A", "first4", (P, BOXES), F32))
        make_h(1, 1)
        make_x(1, 1, stage_tile("E", "first5", (P, BOXES), F32))
        make_h(1, 2)
        make_x(1, 2, plane_tile("first6"))
        make_h(1, 3)
        x_bf0 = stage_tile("A", "x_bf0")
        interleave(nc.scalar.copy, x_bf0[:], x[0][:], 0, BOXES // 4)
        quantize(x_mx[0][0][:], x_mx[0][1][:], x_bf0[:])
        make_x(1, 3, stage_tile("A", "first7", (P, BOXES), F32))

        w3_bf = {}
        for a, place in ((0, "C"), (1, "E")):
            w3_bf[a, 0] = stage_tile(place, f"w3_bf{a}0")
            deal_weight(nc.scalar.copy, w3_bf[a, 0], w3_sb[a, 0])
        x_bf1 = stage_tile("B", "x_bf1")
        interleave_on_both(x_bf1[:], x[1][:], BOXES)
        quantize(x_mx[1][0][:], x_mx[1][1][:], x_bf1[:])
        w3_codes0 = stage_tile("A", "w3_codes0", (P, 2 * GROUP), U32)
        w3_mx = {}
        for a in range(2):
            scales = keep.tile([P, GROUP], U8, name=f"w3_scales{a}0", align_bytes=64)
            w3_mx[a, 0] = (w3_codes0[:, GROUP * a : GROUP * (a + 1)], scales)
            w3_mx[a, 1] = mx_tiles(f"w3_mx{a}1")

        th_banks = [bank_tile(f"th_bank{s}") for s in range(8)]

        def fp4_pass(s, a):
            nc.tensor.matmul_mx(
                out=th_banks[s][:],
                lhsT=w2_codes[:, a, 2 * P * s : 2 * P * (s + 1)].bitcast(FP4X4),
                lhsT_scale=w2_bytes[:, a, P * s : P * (s + 1)],
                rhs=x_mx[a][0][:].bitcast(FP8X4),
                rhs_scale=x_mx[a][1][:],
                start=(a == 0),
                stop=(a == 1),
            )

        for s in range(8):
            fp4_pass(s, 0)
        th = [planes_tile(f"th{g}") for g in range(2)]
        gained = [load_tile(1 - g, 0, f"gained{g}", BF16) for g in range(2)]
        for s in range(8):
            g, t = divmod(s, 4)
            fp4_pass(s, 1)
            nc.scalar.activation(out=th[g][:, t, :], in_=th_banks[s][:], func=ACT.Tanh)
            nc.vector.tensor_scalar(gained[g][:, t, :], th[g][:, t, :], gain_sb[:, g, t : t + 1], None, ALU.mult)
        for a in range(2):
            quantize(w3_mx[a, 0][0][:], w3_mx[a, 0][1][:], w3_bf[a, 0][:])
        gained_mx = [mx_tiles(f"gained_mx{g}") for g in range(2)]
        for g, place in ((0, "D"), (1, "C")):
            gained_bf = stage_tile(place, f"gained_bf{g}")
            half = BOXES // 2
            for u in range(2):
                interleave(nc.vector.tensor_copy, gained_bf[:], gained[g][:], half // 4 * u, half // 4 * (u + 1))
            for u in range(2):
                cols = slice(half * u, half * (u + 1))
                quantize(gained_mx[g][0][:, cols], gained_mx[g][1][:, cols], gained_bf[:, 4 * half * u : 4 * half * (u + 1)])

        y_codes = [keep.tile([P, BUNDLES], U32, name=f"y_codes{g}", align_bytes=64) for g in range(2)]
        y_scales = keep.tile([P, 2, BUNDLES], U8, name="y_scales", align_bytes=64)
        y = [wide_tile([P, 4, BUNDLES], F32, f"y{g}") for g in range(2)]

        def make_box(g):
            banks = [bank_tile(f"box_bank{g}{t}") for t in range(4)]
            for t in range(4):
                fp8_pass(banks[t], w3_mx[0, g], t, gained_mx[0][0][:], gained_mx[0][1][:], 0)
            diffs = []

            def cap(t):
                nc.vector.tensor_scalar(box[4 * g + t][:, 0:BOXES], diffs[t][:], lim_sb[:, g, t : t + 1], None, ALU.min)

            for t in range(4):
                fp8_pass(banks[t], w3_mx[1, g], t, gained_mx[1][0][:], gained_mx[1][1][:], 1)
                diffs.append(plane_tile(f"diff{g}{t}"))
                nc.vector.tensor_tensor(diffs[t][:], banks[t][:], th[g][:, t, :], ALU.subtract)
                if t > 0:
                    cap(t - 1)
            cap(3)

        def scale_h(g, u):
            own = load_tile(1, u, f"own{g}{u}")
            for t in range(4):
                nc.scalar.activation(
                    out=own[:, t, :],
                    in_=h[4 * g + t][:, GROUP * u : GROUP * (u + 1)],
                    func=ACT.Copy,
                    scale=wh_sb[:, g, t : t + 1],
                )
            return own

        def make_y(g, own, c0, c1):
            for t in range(4):
                nc.vector.tensor_tensor(
                    y[g][:, t, c0:c1],
                    box[4 * g + t][:].indirect(pos3_sb[:, c0 // 16 : c1 // 16]),
                    own[:, t, c0 % GROUP : c0 % GROUP + c1 - c0],
                    ALU.add,
                )
            rows = out_0[GROUP * g : GROUP * (g + 1), :].rearrange("(p t) j -> p t j", t=4)
            nc.sync.dma_start(out=rows[:, :, c0:c1], in_=y[g][:, :, c0:c1])

        def quantize_y(g, place, c0, c1, on_both=False):
            y_bf = stage_tile(place, f"y_bf{g}_{c0}", (P, 4 * (c1 - c0)))
            if on_both:
                interleave_on_both(y_bf[:], y[g][:, :, c0:c1], c1 - c0)
            else:
                interleave(nc.scalar.copy, y_bf[:], y[g][:, :, c0:c1], 0, (c1 - c0) // 4)
            quantize(y_codes[g][:, c0:c1], y_scales[:, g, c0:c1], y_bf[:])
            words = out_1[g].rearrange("p m t -> p (m t)").bitcast(I32)
            nc.sync.dma_start(out=words[:, c0:c1], in_=y_codes[g][:, c0:c1].bitcast(I32))

        half, three_quarters = BUNDLES // 2, 3 * BUNDLES // 4
        make_box(0)
        make_y(0, scale_h(0, 0), 0, half)
        for a, place in ((0, "D"), (1, "C")):
            w3_bf[a, 1] = stage_tile(place, f"w3_bf{a}1")
            deal_weight(nc.scalar.copy, w3_bf[a, 1], w3_sb[a, 1])
            quantize(w3_mx[a, 1][0][:], w3_mx[a, 1][1][:], w3_bf[a, 1][:])
        make_y(0, scale_h(0, 1), half, BUNDLES)
        make_box(1)
        quantize_y(0, "A", 0, half)
        make_y(1, scale_h(1, 0), 0, half)
        quantize_y(0, "B", half, BUNDLES)
        own_last = scale_h(1, 1)
        make_y(1, own_last, half, three_quarters)
        quantize_y(1, "A", 0, half)
        make_y(1, own_last, three_quarters, BUNDLES)
        quantize_y(1, "B", half, three_quarters)
        quantize_y(1, "D", three_quarters, BUNDLES, on_both=True)
        for quad in range(4):
            queue = nc.sync if quad % 2 == 0 else nc.scalar
            queue.dma_start(
                out=out_2[:, 4 * quad : 4 * quad + 4, :].rearrange("g r m -> r g m").bitcast(I32),
                in_=y_scales[32 * quad : 32 * quad + 4, :, :].bitcast(I32),
            )
